import numpy as np
import ml_dtypes


def mxq(x, axis, fmt="e4m3"):
    dtype, down = {"e4m3": (ml_dtypes.float8_e4m3fn, 7), "e5m2": (ml_dtypes.float8_e5m2, 14)}[fmt]
    v = np.moveaxis(np.asarray(x, np.float32).astype(ml_dtypes.bfloat16).astype(np.float64), axis, -1)
    blocks = v.reshape(v.shape[:-1] + (-1, 32))
    amax = np.abs(blocks).max(-1, keepdims=True)
    byte = np.maximum(np.where(amax > 0, np.frexp(amax)[1] - 1 + 127, 0) - down, 1)
    scale = np.exp2(byte - 127.0)
    codes = (blocks / scale).astype(np.float32).astype(dtype).astype(np.float64)
    return np.moveaxis((codes * scale).reshape(v.shape), -1, axis)


WIDE = False


def mx_kscale(k):
    if not WIDE:
        return np.ones(k)
    levels = np.array([10, -10, 5, -5, 0])
    if k % 512:
        return np.exp2(np.random.permutation(np.resize(levels, k // 32))).repeat(32)
    a = np.empty((k // 512, 16))
    for p in range(k // 512):
        a[p, :8] = np.random.permutation(np.resize(levels, 8))
        for g in range(8):
            far = levels[np.abs(levels - a[p, g]) >= 10]
            a[p, g + 8] = far[np.random.randint(len(far))]
    return np.exp2(a.ravel()).repeat(32)


def f64(x):
    return np.asarray(x).astype(np.float64)


def striped(idx):
    return np.tile(idx.reshape(-1, 16).T, (8, 1)).astype(np.uint16)


def unstriped(offs):
    return offs[:16].T.reshape(-1).astype(np.int64)


K, T, E, C, N = 128, 4096, 2, 1024, 256


def setup_inputs():
    n = np.random.standard_normal
    idx = np.random.permutation(T)[:E * C]
    s = mx_kscale(E * C)[None, :]
    xT = n((K, T)); dyT = n((N, T))
    xT[:, idx] *= s; dyT[:, idx] /= s
    return {
        "xT": xT.astype(np.float32),
        "dyT": dyT.astype(np.float32),
        "gate": np.tile(np.random.uniform(0.2, 1.0, E * C), (N, 1)).astype(np.float32),
        "offs": striped(idx),
    }


def reference(xT, dyT, gate, offs):
    idx = unstriped(offs)
    xq = mxq(f64(xT)[:, idx], 1, "e4m3")
    gq = mxq(f64(gate) * f64(dyT)[:, idx], 1, "e4m3")
    return np.stack([(xq[:, e * C:(e + 1) * C] @ gq[:, e * C:(e + 1) * C].T) for e in range(E)])

@@ -1,0 +1,137 @@
+from contextlib import ExitStack
+
+import concourse.mybir as mybir
+from concourse.masks import make_identity
+
+K, T, E, C, N = 128, 4096, 2, 1024, 256
+S = E * C
+P = 128
+PASS = 512
+PASSES = S // PASS
+FLOPS = 2 * S * K * N
+
+F32 = mybir.dt.float32
+BF16 = mybir.dt.bfloat16
+U32 = mybir.dt.uint32
+U16 = mybir.dt.uint16
+U8 = mybir.dt.uint8
+FP8X4 = mybir.dt.float8_e4m3fn_x4
+MULT = mybir.AluOpType.mult
+
+
+def tile_moe_bdw_lin_none_kernel(tc, xT, dyT, gate, offs, out):
+    nc = tc.nc
+    with ExitStack() as ctx:
+        held = ctx.enter_context(tc.tile_pool(name="held", bufs=1))
+        turn_pool = ctx.enter_context(tc.psum_pool(name="turn", bufs=4))
+        acc_pool = ctx.enter_context(tc.psum_pool(name="acc", bufs=1))
+
+        offsets = held.tile([P, S // 16], U16, name="offsets")
+        nc.sync.dma_start(offsets[:], offs)
+
+        x_all = held.tile([P, T], F32, name="x_all")
+        dy_all = [held.tile([P, T], F32, name=f"dy_all{h}") for h in range(2)]
+        gates = held.tile([P, S], F32, name="gates")
+
+        gate_rows = held.tile([P, P], F32, name="gate_rows")
+        nc.vector.memset(gate_rows[:], 0.0)
+        nc.sync.dma_start(gate_rows[0:16, :], gate[0:1, :].rearrange("o (c n) -> (o c) n", n=P))
+        nc.sync.dma_start(x_all[:], xT)
+        nc.sync.dma_start(dy_all[0][:], dyT[0:P, :])
+        nc.sync.dma_start(dy_all[1][:], dyT[P : 2 * P, :])
+
+        identity = held.tile([P, P], F32, name="identity")
+        make_identity(nc, identity[:])
+        warm = held.tile([P, 1], F32, name="warm")
+        nc.scalar.copy(out=warm[:], in_=identity[:, 0:1])
+
+        bank = turn_pool.tile([P, 4, P], F32, name="bank")
+        nc.tensor.transpose(bank[:, 0, :], gate_rows[:], identity[:])
+        gate_cols = held.tile([P, 16], F32, name="gate_cols")
+        nc.scalar.copy(out=gate_cols[:], in_=bank[:, 0, 0:16])
+        for b in range(4):
+            bank = turn_pool.tile([P, 4, P], F32, name="bank")
+            for c in range(4):
+                j = 4 * b + c
+                nc.tensor.transpose(bank[:, c, :], gate_cols[:, j : j + 1].to_broadcast([P, P]), identity[:])
+            nc.scalar.copy(out=gates[:, b * 512 : (b + 1) * 512], in_=bank[:].rearrange("p c n -> p (c n)"))
+
+        picked = [held.tile([P, S], F32, name=f"picked{s}") for s in range(3)]
+        rows = [held.tile([P, PASSES, P, 4], BF16, align_bytes=64, name=f"rows{s}") for s in range(3)]
+        codes = [held.tile([P, S // 4], U32, align_bytes=64, name=f"codes{s}") for s in range(3)]
+        scales = [held.tile([P, S // 4], U8, align_bytes=64, name=f"scales{s}") for s in range(3)]
+
+        def gather(s, a, b):
+            lst = offsets[:, a // 16 : b // 16]
+            if s == 0:
+                nc.vector.tensor_copy(picked[s][:, a:b], x_all[:].indirect(lst))
+            else:
+                nc.vector.tensor_tensor(picked[s][:, a:b], dy_all[s - 1][:].indirect(lst), gates[:, a:b], MULT)
+
+        def turn(s, q):
+            bank = turn_pool.tile([P, 4, P], F32, name="bank")
+            for t in range(4):
+                nc.tensor.transpose(bank[:, t, :], picked[s][:, q * PASS + t : (q + 1) * PASS : 4], identity[:])
+            nc.scalar.copy(out=rows[s][:, q, :, :], in_=bank[:].rearrange("p t n -> p n t"))
+
+        def quantize(s, q0, q1):
+            cols = slice(q0 * P, q1 * P)
+            nc.vector.quantize_mx(
+                out=codes[s][:, cols].bitcast(FP8X4),
+                scales=scales[s][:, cols],
+                in_=rows[s][:, q0:q1, :, :].rearrange("p q n t -> p (q n t)"),
+            )
+
+        accs = {}
+
+        def multiply(h, q):
+            e = q // 2
+            if q % 2 == 0:
+                accs[h, e] = acc_pool.tile([P, P], F32, name=f"acc{h}{e}")
+            acc = accs[h, e]
+            cols = slice(q * P, (q + 1) * P)
+            nc.tensor.matmul_mx(
+                out=acc[:],
+                lhsT=codes[0][:, cols].bitcast(FP8X4),
+                lhsT_scale=scales[0][:, cols],
+                rhs=codes[h + 1][:, cols].bitcast(FP8X4),
+                rhs_scale=scales[h + 1][:, cols],
+                start=(q % 2 == 0),
+                stop=(q % 2 == 1),
+            )
+            if q % 2 == 1:
+                res = held.tile([P, P], F32, name=f"res{h}{e}")
+                nc.scalar.copy(out=res[:], in_=acc[:])
+                nc.sync.dma_start(out[e, :, h * P : (h + 1) * P], res[:])
+
+        gather(0, 0, 1024)
+        turn(0, 0)
+        turn(0, 1)
+        gather(0, 1024, 2048)
+        turn(0, 2)
+        turn(0, 3)
+        gather(1, 0, 512)
+        turn(1, 0)
+        gather(1, 512, 1024)
+        turn(1, 1)
+        quantize(0, 0, 4)
+        gather(1, 1024, 2048)
+        turn(1, 2)
+        turn(1, 3)
+        gather(2, 0, 1024)
+        turn(2, 0)
+        turn(2, 1)
+        quantize(1, 0, 4)
+        for q in range(4):
+            multiply(0, q)
+        gather(2, 1024, 1536)
+        turn(2, 2)
+        quantize(2, 0, 2)
+        multiply(1, 0)
+        multiply(1, 1)
+        gather(2, 1536, 2048)
+        turn(2, 3)
+        quantize(2, 2, 3)
+        multiply(1, 2)
+        quantize(2, 3, 4)
+        multiply(1, 3)

@@ -34,8 +34,7 @@ def tile_moe_bdw_lin_none_kernel(tc, xT, dyT, gate, offs, out):
         gates = held.tile([P, S], F32, name="gates")
 
         gate_rows = held.tile([P, P], F32, name="gate_rows")
-        nc.vector.memset(gate_rows[:], 0.0)
-        nc.sync.dma_start(gate_rows[0:16, :], gate[0:1, :].rearrange("o (c n) -> (o c) n", n=P))
+        nc.scalar.dma_start(gate_rows[:], gate[0:8, :].rearrange("o (c n) -> (o c) n", n=P))
         nc.sync.dma_start(x_all[:], xT)
         nc.sync.dma_start(dy_all[0][:], dyT[0:P, :])
         nc.sync.dma_start(dy_all[1][:], dyT[P : 2 * P, :])
@@ -58,7 +57,9 @@ def tile_moe_bdw_lin_none_kernel(tc, xT, dyT, gate, offs, out):
 
         picked = [held.tile([P, S], F32, name=f"picked{s}") for s in range(3)]
         rows = [held.tile([P, PASSES, P, 4], BF16, align_bytes=64, name=f"rows{s}") for s in range(3)]
-        codes = [held.tile([P, S // 4], U32, align_bytes=64, name=f"codes{s}") for s in range(3)]
+        codes = [held.tile([P, 4, P], U32, align_bytes=64, name="codes0")]
+        last = held.tile([P, PASS], F32, name="last", tag="late", align_bytes=64)
+        last_half = held.tile([P, PASS], BF16, name="last_half", align_bytes=64)
         scales = [held.tile([P, S // 4], U8, align_bytes=64, name=f"scales{s}") for s in range(3)]
 
         def gather(s, a, b):
@@ -66,7 +67,7 @@ def tile_moe_bdw_lin_none_kernel(tc, xT, dyT, gate, offs, out):
             if s == 0:
                 nc.vector.tensor_copy(picked[s][:, a:b], x_all[:].indirect(lst))
             else:
-                nc.vector.tensor_tensor(picked[s][:, a:b], dy_all[s - 1][:].indirect(lst), gates[:, a:b], MULT)
+                nc.vector.tensor_tensor(last[:] if (s, a) == (2, 1536) else picked[s][:, a:b], dy_all[s - 1][:].indirect(lst), gates[:, a:b], MULT)
 
         def turn(s, q):
             bank = turn_pool.tile([P, 4, P], F32, name="bank")
@@ -74,10 +75,24 @@ def tile_moe_bdw_lin_none_kernel(tc, xT, dyT, gate, offs, out):
                 nc.tensor.transpose(bank[:, t, :], picked[s][:, q * PASS + t : (q + 1) * PASS : 4], identity[:])
             nc.scalar.copy(out=rows[s][:, q, :, :], in_=bank[:].rearrange("p t n -> p n t"))
 
+        def turn_last():
+            nc.vector.tensor_copy(
+                out=last_half[:].rearrange("f (u p e) -> f u p e", u=2, e=2),
+                in_=last[:].rearrange("f (p u e) -> f u p e", u=2, e=2),
+            )
+            words = last_half[:].bitcast(F32)
+            bank = turn_pool.tile([P, 2, P], F32, name="bank")
+            for u in range(2):
+                nc.tensor.transpose(bank[:, u, :], words[:, u * P : (u + 1) * P], identity[:])
+            nc.scalar.copy(
+                out=rows[2][:, 3, :, :].rearrange("p n t -> p (n t)").bitcast(F32).rearrange("p (n u) -> p n u", u=2),
+                in_=bank[:].rearrange("p u n -> p n u"),
+            )
+
         def quantize(s, q0, q1):
             cols = slice(q0 * P, q1 * P)
             nc.vector.quantize_mx(
-                out=codes[s][:, cols].bitcast(FP8X4),
+                out=codes[s][:, q0:q1, :].rearrange("p q n -> p (q n)").bitcast(FP8X4),
                 scales=scales[s][:, cols],
                 in_=rows[s][:, q0:q1, :, :].rearrange("p q n t -> p (q n t)"),
             )
@@ -92,9 +107,9 @@ def tile_moe_bdw_lin_none_kernel(tc, xT, dyT, gate, offs, out):
             cols = slice(q * P, (q + 1) * P)
             nc.tensor.matmul_mx(
                 out=acc[:],
-                lhsT=codes[0][:, cols].bitcast(FP8X4),
+                lhsT=codes[0][:, q, :].bitcast(FP8X4),
                 lhsT_scale=scales[0][:, cols],
-                rhs=codes[h + 1][:, cols].bitcast(FP8X4),
+                rhs=codes[h + 1][:, q, :].bitcast(FP8X4),
                 rhs_scale=scales[h + 1][:, cols],
                 start=(q % 2 == 0),
                 stop=(q % 2 == 1),
@@ -110,9 +125,8 @@ def tile_moe_bdw_lin_none_kernel(tc, xT, dyT, gate, offs, out):
         gather(0, 1024, 2048)
         turn(0, 2)
         turn(0, 3)
-        gather(1, 0, 512)
+        gather(1, 0, 1024)
         turn(1, 0)
-        gather(1, 512, 1024)
         turn(1, 1)
         quantize(0, 0, 4)
         gather(1, 1024, 2048)
@@ -121,17 +135,19 @@ def tile_moe_bdw_lin_none_kernel(tc, xT, dyT, gate, offs, out):
         gather(2, 0, 1024)
         turn(2, 0)
         turn(2, 1)
-        quantize(1, 0, 4)
-        for q in range(4):
-            multiply(0, q)
         gather(2, 1024, 1536)
         turn(2, 2)
+        gather(2, 1536, 2048)
+        turn_last()
+        late = held.tile([P, 2, 4, P], U32, name="late", tag="late", align_bytes=64)
+        codes.extend([late[:, 0, :, :], late[:, 1, :, :]])
+        quantize(1, 0, 4)
         quantize(2, 0, 2)
+        quantize(2, 2, 3)
+        for q in range(4):
+            multiply(0, q)
         multiply(1, 0)
         multiply(1, 1)
-        gather(2, 1536, 2048)
-        turn(2, 3)
-        quantize(2, 2, 3)
         multiply(1, 2)
         quantize(2, 3, 4)
         multiply(1, 3)

@@ -34,7 +34,9 @@ def tile_moe_bdw_lin_none_kernel(tc, xT, dyT, gate, offs, out):
         gates = held.tile([P, S], F32, name="gates")
 
         gate_rows = held.tile([P, P], F32, name="gate_rows")
-        nc.scalar.dma_start(gate_rows[:], gate[0:8, :].rearrange("o (c n) -> (o c) n", n=P))
+        nc.gpsimd.memset(gate_rows[32:64, :], 0.0)
+        nc.gpsimd.memset(gate_rows[64:P, :], 0.0)
+        nc.scalar.dma_start(gate_rows[0:32, :], gate[0:2, :].rearrange("o (c n) -> (o c) n", n=P))
         nc.sync.dma_start(x_all[:], xT)
         nc.sync.dma_start(dy_all[0][:], dyT[0:P, :])
         nc.sync.dma_start(dy_all[1][:], dyT[P : 2 * P, :])
@@ -59,7 +61,7 @@ def tile_moe_bdw_lin_none_kernel(tc, xT, dyT, gate, offs, out):
         rows = [held.tile([P, PASSES, P, 4], BF16, align_bytes=64, name=f"rows{s}") for s in range(3)]
         codes = [held.tile([P, 4, P], U32, align_bytes=64, name="codes0")]
         last = held.tile([P, PASS], F32, name="last", tag="late", align_bytes=64)
-        last_half = held.tile([P, PASS], BF16, name="last_half", align_bytes=64)
+        halves = [held.tile([P, w], BF16, name=f"half{w}{i}", align_bytes=64) for i, w in enumerate((1024, 512, 512))]
         scales = [held.tile([P, S // 4], U8, align_bytes=64, name=f"scales{s}") for s in range(3)]
 
         def gather(s, a, b):
@@ -75,18 +77,16 @@ def tile_moe_bdw_lin_none_kernel(tc, xT, dyT, gate, offs, out):
                 nc.tensor.transpose(bank[:, t, :], picked[s][:, q * PASS + t : (q + 1) * PASS : 4], identity[:])
             nc.scalar.copy(out=rows[s][:, q, :, :], in_=bank[:].rearrange("p t n -> p n t"))
 
-        def turn_last():
-            nc.vector.tensor_copy(
-                out=last_half[:].rearrange("f (u p e) -> f u p e", u=2, e=2),
-                in_=last[:].rearrange("f (p u e) -> f u p e", u=2, e=2),
-            )
-            words = last_half[:].bitcast(F32)
-            bank = turn_pool.tile([P, 2, P], F32, name="bank")
-            for u in range(2):
-                nc.tensor.transpose(bank[:, u, :], words[:, u * P : (u + 1) * P], identity[:])
+        def turn_words(src, half, q0, q1, cast):
+            cast(out=half[:], in_=src)
+            words = half[:].bitcast(F32)
+            bank = turn_pool.tile([P, q1 - q0, 2, P], F32, name="bank")
+            for q in range(q1 - q0):
+                for u in range(2):
+                    nc.tensor.transpose(bank[:, q, u, :], words[:, q * 256 + u : (q + 1) * 256 : 2], identity[:])
             nc.scalar.copy(
-                out=rows[2][:, 3, :, :].rearrange("p n t -> p (n t)").bitcast(F32).rearrange("p (n u) -> p n u", u=2),
-                in_=bank[:].rearrange("p u n -> p n u"),
+                out=rows[2][:, q0:q1, :, :].rearrange("p q n t -> p (q n t)").bitcast(F32).rearrange("p (q n u) -> p q n u", q=q1 - q0, u=2),
+                in_=bank[:].rearrange("p q u n -> p q n u"),
             )
 
         def quantize(s, q0, q1):
@@ -133,12 +133,11 @@ def tile_moe_bdw_lin_none_kernel(tc, xT, dyT, gate, offs, out):
         turn(1, 2)
         turn(1, 3)
         gather(2, 0, 1024)
-        turn(2, 0)
-        turn(2, 1)
+        turn_words(picked[2][:, 0:1024], halves[0], 0, 2, nc.scalar.copy)
         gather(2, 1024, 1536)
-        turn(2, 2)
+        turn_words(picked[2][:, 1024:1536], halves[1], 2, 3, nc.scalar.copy)
         gather(2, 1536, 2048)
-        turn_last()
+        turn_words(last[:], halves[2], 3, 4, nc.vector.tensor_copy)
         late = held.tile([P, 2, 4, P], U32, name="late", tag="late", align_bytes=64)
         codes.extend([late[:, 0, :, :], late[:, 1, :, :]])
         quantize(1, 0, 4)

@@ -30,7 +30,7 @@ def tile_moe_bdw_lin_none_kernel(tc, xT, dyT, gate, offs, out):
         nc.sync.dma_start(offsets[:], offs)
 
         x_all = held.tile([P, T], F32, name="x_all")
-        dy_all = [held.tile([P, T], F32, name=f"dy_all{h}") for h in range(2)]
+        dy_all = [held.tile([P, T], F32, name="dy_all0"), held.tile([P, T], F32, name="dy_all1", tag="late", align_bytes=64)]
         gates = held.tile([P, S], F32, name="gates")
 
         gate_rows = held.tile([P, P], F32, name="gate_rows")
@@ -59,9 +59,8 @@ def tile_moe_bdw_lin_none_kernel(tc, xT, dyT, gate, offs, out):
 
         picked = [held.tile([P, S], F32, name=f"picked{s}") for s in range(3)]
         rows = [held.tile([P, PASSES, P, 4], BF16, align_bytes=64, name=f"rows{s}") for s in range(3)]
-        codes = [held.tile([P, 4, P], U32, align_bytes=64, name="codes0")]
-        last = held.tile([P, PASS], F32, name="last", tag="late", align_bytes=64)
-        halves = [held.tile([P, w], BF16, name=f"half{w}{i}", align_bytes=64) for i, w in enumerate((1024, 512, 512))]
+        codes = []
+        half = held.tile([P, PASS], BF16, name="half", align_bytes=64)
         scales = [held.tile([P, S // 4], U8, align_bytes=64, name=f"scales{s}") for s in range(3)]
 
         def gather(s, a, b):
@@ -69,7 +68,7 @@ def tile_moe_bdw_lin_none_kernel(tc, xT, dyT, gate, offs, out):
             if s == 0:
                 nc.vector.tensor_copy(picked[s][:, a:b], x_all[:].indirect(lst))
             else:
-                nc.vector.tensor_tensor(last[:] if (s, a) == (2, 1536) else picked[s][:, a:b], dy_all[s - 1][:].indirect(lst), gates[:, a:b], MULT)
+                nc.vector.tensor_tensor(picked[s][:, a:b], dy_all[s - 1][:].indirect(lst), gates[:, a:b], MULT)
 
         def turn(s, q):
             bank = turn_pool.tile([P, 4, P], F32, name="bank")
@@ -128,18 +127,19 @@ def tile_moe_bdw_lin_none_kernel(tc, xT, dyT, gate, offs, out):
         gather(1, 0, 1024)
         turn(1, 0)
         turn(1, 1)
-        quantize(0, 0, 4)
         gather(1, 1024, 2048)
         turn(1, 2)
         turn(1, 3)
         gather(2, 0, 1024)
-        turn_words(picked[2][:, 0:1024], halves[0], 0, 2, nc.scalar.copy)
+        turn(2, 0)
+        turn(2, 1)
         gather(2, 1024, 1536)
-        turn_words(picked[2][:, 1024:1536], halves[1], 2, 3, nc.scalar.copy)
+        turn(2, 2)
         gather(2, 1536, 2048)
-        turn_words(last[:], halves[2], 3, 4, nc.vector.tensor_copy)
-        late = held.tile([P, 2, 4, P], U32, name="late", tag="late", align_bytes=64)
-        codes.extend([late[:, 0, :, :], late[:, 1, :, :]])
+        turn_words(picked[2][:, 1536:2048], half, 3, 4, nc.scalar.copy)
+        late = held.tile([P, 3, 4, P], U32, name="late", tag="late", align_bytes=64)
+        codes.extend([late[:, s, :, :] for s in range(3)])
+        quantize(0, 0, 4)
         quantize(1, 0, 4)
         quantize(2, 0, 2)
         quantize(2, 2, 3)

from contextlib import ExitStack

import concourse.mybir as mybir
from concourse.masks import make_identity

K, T, E, C, N = 128, 4096, 2, 1024, 256
S = E * C
P = 128
PASS = 512
PASSES = S // PASS
FLOPS = 2 * S * K * N

F32 = mybir.dt.float32
BF16 = mybir.dt.bfloat16
U32 = mybir.dt.uint32
U16 = mybir.dt.uint16
U8 = mybir.dt.uint8
FP8X4 = mybir.dt.float8_e4m3fn_x4
MULT = mybir.AluOpType.mult


def tile_moe_bdw_lin_none_kernel(tc, xT, dyT, gate, offs, out):
    nc = tc.nc
    with ExitStack() as ctx:
        held = ctx.enter_context(tc.tile_pool(name="held", bufs=1))
        turn_pool = ctx.enter_context(tc.psum_pool(name="turn", bufs=4))
        acc_pool = ctx.enter_context(tc.psum_pool(name="acc", bufs=1))

        offsets = held.tile([P, S // 16], U16, name="offsets")
        nc.sync.dma_start(offsets[:], offs)

        x_all = held.tile([P, T], F32, name="x_all")
        dy_all = [held.tile([P, T], F32, name="dy_all0"), held.tile([P, T], F32, name="dy_all1", tag="late", align_bytes=64)]
        gates = held.tile([P, S], F32, name="gates")

        gate_rows = held.tile([P, P], F32, name="gate_rows")
        nc.gpsimd.memset(gate_rows[32:64, :], 0.0)
        nc.gpsimd.memset(gate_rows[64:P, :], 0.0)
        nc.scalar.dma_start(gate_rows[0:32, :], gate[0:2, :].rearrange("o (c n) -> (o c) n", n=P))
        nc.sync.dma_start(x_all[:], xT)
        nc.sync.dma_start(dy_all[0][:], dyT[0:P, :])
        nc.sync.dma_start(dy_all[1][:], dyT[P : 2 * P, :])

        identity = held.tile([P, P], F32, name="identity")
        make_identity(nc, identity[:])
        warm = held.tile([P, 1], F32, name="warm")
        nc.scalar.copy(out=warm[:], in_=identity[:, 0:1])

        bank = turn_pool.tile([P, 4, P], F32, name="bank")
        nc.tensor.transpose(bank[:, 0, :], gate_rows[:], identity[:])
        gate_cols = held.tile([P, 16], F32, name="gate_cols")
        nc.scalar.copy(out=gate_cols[:], in_=bank[:, 0, 0:16])
        for b in range(4):
            bank = turn_pool.tile([P, 4, P], F32, name="bank")
            for c in range(4):
                j = 4 * b + c
                nc.tensor.transpose(bank[:, c, :], gate_cols[:, j : j + 1].to_broadcast([P, P]), identity[:])
            nc.scalar.copy(out=gates[:, b * 512 : (b + 1) * 512], in_=bank[:].rearrange("p c n -> p (c n)"))

        picked = [held.tile([P, S], F32, name=f"picked{s}") for s in range(3)]
        rows = [held.tile([P, PASSES, P, 4], BF16, align_bytes=64, name=f"rows{s}") for s in range(3)]
        codes = []
        half = held.tile([P, PASS], BF16, name="half", align_bytes=64)
        scales = [held.tile([P, S // 4], U8, align_bytes=64, name=f"scales{s}") for s in range(3)]

        def gather(s, a, b):
            lst = offsets[:, a // 16 : b // 16]
            if s == 0:
                nc.vector.tensor_copy(picked[s][:, a:b], x_all[:].indirect(lst))
            else:
                nc.vector.tensor_tensor(picked[s][:, a:b], dy_all[s - 1][:].indirect(lst), gates[:, a:b], MULT)

        def turn(s, q):
            bank = turn_pool.tile([P, 4, P], F32, name="bank")
            for t in range(4):
                nc.tensor.transpose(bank[:, t, :], picked[s][:, q * PASS + t : (q + 1) * PASS : 4], identity[:])
            nc.scalar.copy(out=rows[s][:, q, :, :], in_=bank[:].rearrange("p t n -> p n t"))

        def turn_words(src, half, q0, q1, cast):
            cast(out=half[:], in_=src)
            words = half[:].bitcast(F32)
            bank = turn_pool.tile([P, q1 - q0, 2, P], F32, name="bank")
            for q in range(q1 - q0):
                for u in range(2):
                    nc.tensor.transpose(bank[:, q, u, :], words[:, q * 256 + u : (q + 1) * 256 : 2], identity[:])
            nc.scalar.copy(
                out=rows[2][:, q0:q1, :, :].rearrange("p q n t -> p (q n t)").bitcast(F32).rearrange("p (q n u) -> p q n u", q=q1 - q0, u=2),
                in_=bank[:].rearrange("p q u n -> p q n u"),
            )

        def quantize(s, q0, q1):
            cols = slice(q0 * P, q1 * P)
            nc.vector.quantize_mx(
                out=codes[s][:, q0:q1, :].rearrange("p q n -> p (q n)").bitcast(FP8X4),
                scales=scales[s][:, cols],
                in_=rows[s][:, q0:q1, :, :].rearrange("p q n t -> p (q n t)"),
            )

        accs = {}

        def multiply(h, q):
            e = q // 2
            if q % 2 == 0:
                accs[h, e] = acc_pool.tile([P, P], F32, name=f"acc{h}{e}")
            acc = accs[h, e]
            cols = slice(q * P, (q + 1) * P)
            nc.tensor.matmul_mx(
                out=acc[:],
                lhsT=codes[0][:, q, :].bitcast(FP8X4),
                lhsT_scale=scales[0][:, cols],
                rhs=codes[h + 1][:, q, :].bitcast(FP8X4),
                rhs_scale=scales[h + 1][:, cols],
                start=(q % 2 == 0),
                stop=(q % 2 == 1),
            )
            if q % 2 == 1:
                res = held.tile([P, P], F32, name=f"res{h}{e}")
                nc.scalar.copy(out=res[:], in_=acc[:])
                nc.sync.dma_start(out[e, :, h * P : (h + 1) * P], res[:])

        gather(0, 0, 1024)
        turn(0, 0)
        turn(0, 1)
        gather(0, 1024, 2048)
        turn(0, 2)
        turn(0, 3)
        gather(1, 0, 1024)
        turn(1, 0)
        turn(1, 1)
        gather(1, 1024, 2048)
        turn(1, 2)
        turn(1, 3)
        gather(2, 0, 1024)
        turn(2, 0)
        turn(2, 1)
        gather(2, 1024, 1536)
        turn(2, 2)
        gather(2, 1536, 2048)
        turn_words(picked[2][:, 1536:2048], half, 3, 4, nc.scalar.copy)
        late = held.tile([P, 3, 4, P], U32, name="late", tag="late", align_bytes=64)
        codes.extend([late[:, s, :, :] for s in range(3)])
        quantize(0, 0, 4)
        quantize(1, 0, 4)
        quantize(2, 0, 2)
        quantize(2, 2, 3)
        for q in range(4):
            multiply(0, q)
        multiply(1, 0)
        multiply(1, 1)
        multiply(1, 2)
        quantize(2, 3, 4)
        multiply(1, 3)
